import numpy as np
import ml_dtypes


def mxq(x, axis, fmt="e4m3"):
    dtype, down = {"e4m3": (ml_dtypes.float8_e4m3fn, 7), "e5m2": (ml_dtypes.float8_e5m2, 14)}[fmt]
    v = np.moveaxis(np.asarray(x, np.float32).astype(ml_dtypes.bfloat16).astype(np.float64), axis, -1)
    blocks = v.reshape(v.shape[:-1] + (-1, 32))
    amax = np.abs(blocks).max(-1, keepdims=True)
    byte = np.maximum(np.where(amax > 0, np.frexp(amax)[1] - 1 + 127, 0) - down, 1)
    scale = np.exp2(byte - 127.0)
    codes = (blocks / scale).astype(np.float32).astype(dtype).astype(np.float64)
    return np.moveaxis((codes * scale).reshape(v.shape), -1, axis)


WIDE = False


def mx_kscale(k, group=512):
    if not WIDE:
        return np.ones(k)
    levels = np.array([10, -10, 5, -5, 0])
    if group != 512:
        return np.exp2(np.random.permutation(np.resize(levels, k // group))).repeat(group)
    if k % 512:
        return np.exp2(np.random.permutation(np.resize(levels, k // 32))).repeat(32)
    a = np.empty((k // 512, 16))
    for p in range(k // 512):
        a[p, :8] = np.random.permutation(np.resize(levels, 8))
        for g in range(8):
            far = levels[np.abs(levels - a[p, g]) >= 10]
            a[p, g + 8] = far[np.random.randint(len(far))]
    return np.exp2(a.ravel()).repeat(32)


def f64(x):
    return np.asarray(x).astype(np.float64)


def softplus(v):
    return np.log(1.0 + np.exp(v))


def sigmoid(v):
    return 1.0 / (1.0 + np.exp(-v))


def bf(x):
    return np.asarray(x, np.float32).astype(ml_dtypes.bfloat16)


def planes(Y):
    r, m = Y.shape
    b = f64(bf(Y)).reshape(r // 32, 32, m)
    amax = np.abs(b).max(1)
    byte = np.clip(np.where(amax > 0, np.frexp(amax)[1] - 1 + 127 - 7, 1), 1, 254)
    codes = (b * np.exp2(127.0 - byte)[:, None, :]).reshape(r, m).astype(np.float32).astype(ml_dtypes.float8_e4m3fn).view(np.uint8)
    words = codes.reshape(r // 512, 128, 4, m).transpose(0, 1, 3, 2)
    return np.ascontiguousarray(words), np.ascontiguousarray(byte.astype(np.uint8).reshape(r // 512, 16, m))


G, D, M, N = 2, 256, 256, 512


def setup_inputs():
    n = np.random.standard_normal
    s_d = mx_kscale(D, 0)
    return {
        "x": (n((G, D, N)) * s_d[:, None]).astype(np.float32),
        "w1": (n((G, D, M)) / np.sqrt(D) / s_d[:, None]).astype(np.float32),
        "w2": (n((G, D, M)) / np.sqrt(D) / s_d[:, None]).astype(np.float32),
        "re": (np.random.uniform(50.0, 200.0, (G, M, 1))).astype(np.float32),
        "dx": (n((G, D, N)) * s_d[:, None]).astype(np.float32),
        "og": (np.random.uniform(0.5, 2.0, (G, M, 1))).astype(np.float32),
        "base": (0.3 * n((G, M, N))).astype(np.float32),
    }


def reference(x, w1, w2, re, dx, og, base):
    w1q = mxq(f64(w1), 1, "e4m3")
    xq = mxq(f64(x), 1, "e4m3")
    z1 = w1q.transpose(0, 2, 1) @ xq
    dxq = mxq(f64(dx), 1, "e4m3")
    tz1 = w1q.transpose(0, 2, 1) @ dxq
    w2q = mxq(f64(w2), 1, "e4m3")
    z2 = w2q.transpose(0, 2, 1) @ xq
    tz2 = w2q.transpose(0, 2, 1) @ dxq
    p1 = softplus(z1)
    zs = np.sum(p1, axis=-1, keepdims=True) + f64(re)
    xp1 = tz1 * sigmoid(z1)
    xzs = np.sum(xp1, axis=-1, keepdims=True)
    xh = ((xp1 - xzs * p1 / zs) / zs * np.tanh(z2) + tz2 * (1.0 - np.square(np.tanh(z2))) * p1 / zs) * 512.0
    y = xh * f64(og) + f64(base)
    Y = y.reshape(G * M, N)
    words, scales = planes(Y)
    return Y, words, scales

@@ -1,0 +1,262 @@
+from contextlib import ExitStack
+
+import concourse.mybir as mybir
+
+G, D, M, N = 2, 256, 256, 512
+FLOPS = 4 * 2 * G * D * M * N
+
+F32 = mybir.dt.float32
+BF16 = mybir.dt.bfloat16
+I32 = mybir.dt.int32
+U32 = mybir.dt.uint32
+U8 = mybir.dt.uint8
+FP8X4 = mybir.dt.float8_e4m3fn_x4
+ALU = mybir.AluOpType
+ACT = mybir.ActivationFunctionType
+
+P = 128
+PACK = 4
+ROWS = D // PACK
+H = M // P
+HALF = N // 2
+LN_FLOOR = 1e-12
+
+
+def tile_rows_pl_tnrowshare_kernel(tc, x, w1, w2, re, dx, og, base, out_0, out_1, out_2):
+    nc = tc.nc
+    tiles = [(g, h) for g in range(G) for h in range(H)]
+
+    with ExitStack() as ctx:
+        sb = ctx.enter_context(tc.tile_pool(name="sb", bufs=1))
+        ps = ctx.enter_context(tc.psum_pool(name="ps", bufs=1))
+        ctx.enter_context(tc.manual_schedule())
+
+        def tile(name, shape, dtype):
+            return sb.tile(shape, dtype, name=name, tag=name, align_bytes=64)
+
+        def load_k_first(name, src, width):
+            raw = tile(name, [P, PACK, width], F32)
+            nc.sync.dma_start(out=raw[:], in_=src.rearrange("g (p j) w -> (g p) j w", j=PACK))
+            return raw
+
+        x_raw = load_k_first("x_raw", x, N)
+        w1_raw = load_k_first("w1_raw", w1, M)
+        dx_raw = load_k_first("dx_raw", dx, N)
+        w2_raw = load_k_first("w2_raw", w2, M)
+        re_sb = tile("re_sb", [P, G, H], F32)
+        nc.sync.dma_start(out=re_sb[:], in_=re.rearrange("g (q h) o -> q g (h o)", h=H))
+        og_sb = tile("og_sb", [P, G, H], F32)
+        nc.sync.dma_start(out=og_sb[:], in_=og.rearrange("g (q h) o -> q g (h o)", h=H))
+        base_sb = tile("base_sb", [P, G, H * N], F32)
+        nc.sync.dma_start(out=base_sb[:], in_=base.rearrange("g (q h) n -> q g (h n)", h=H))
+
+        def round_columns(name, raw, a):
+            grouped = tile(name, [P, HALF * PACK], BF16)
+            nc.vector.tensor_copy(
+                out=grouped[:].rearrange("p (c i j) -> p c j i", i=4, j=PACK),
+                in_=raw[:, :, a * HALF : (a + 1) * HALF].rearrange("p j (c i) -> p c j i", i=4),
+            )
+            return grouped
+
+        def weight_views(name, raw):
+            grouped = tile(name, [P, M * PACK], BF16)
+            dst = grouped[:].rearrange("p (h c i j) -> p c j i h", h=H, i=2, j=PACK)
+            src = raw[:].rearrange("p j (c i h) -> p c j i h", i=2, h=H)
+            return grouped, dst, src
+
+        def mx_tiles(name, width):
+            return tile(name + "_codes", [P, width], U32), tile(name + "_scales", [P, width], U8)
+
+        def quantise(mx, cols, grouped):
+            nc.vector.quantize_mx(out=mx[0][:, cols].bitcast(FP8X4), scales=mx[1][:, cols], in_=grouped[:])
+
+        banks = [[ps.tile([P, N], F32, name="bank%d%d" % (g, b), tag="bank%d%d" % (g, b)) for b in range(2 * H)] for g in range(G)]
+
+        def product(w_mx, x_mx, first_bank, which):
+            for g, h in which:
+                rows = slice(g * ROWS, (g + 1) * ROWS)
+                cols = slice(h * P, (h + 1) * P)
+                nc.tensor.matmul_mx(
+                    out=banks[g][first_bank + h][:],
+                    lhsT=w_mx[0][rows, cols].bitcast(FP8X4),
+                    lhsT_scale=w_mx[1][rows, cols],
+                    rhs=x_mx[0][rows, :].bitcast(FP8X4),
+                    rhs_scale=x_mx[1][rows, :],
+                    start=True,
+                    stop=True,
+                )
+
+        halves = [slice(a * HALF, (a + 1) * HALF) for a in range(2)]
+        x_mx, dx_mx = mx_tiles("x", N), mx_tiles("dx", N)
+        w1_mx, w2_mx = mx_tiles("w1", M), mx_tiles("w2", M)
+
+        x_b = [round_columns("x_b%d" % a, x_raw, a) for a in range(2)]
+        quantise(x_mx, halves[0], x_b[0])
+        w1_b, w1_dst, w1_src = weight_views("w1_b", w1_raw)
+        nc.vector.tensor_copy(out=w1_dst, in_=w1_src)
+        quantise(x_mx, halves[1], x_b[1])
+        quantise(w1_mx, slice(0, M), w1_b)
+        product(w1_mx, x_mx, 0, tiles)
+
+        dx_b = [round_columns("dx_b%d" % a, dx_raw, a) for a in range(2)]
+        for a in range(2):
+            quantise(dx_mx, halves[a], dx_b[a])
+        product(w1_mx, dx_mx, H, tiles)
+
+        def per_tile(name):
+            return {t: tile("%s%d%d" % (name, t[0], t[1]), [P, N], F32) for t in tiles}
+
+        q, lnq, nxp, p1, a1, t2, tt, gz, u, w, e = [per_tile(n) for n in ("q", "lnq", "nxp", "p", "a", "t", "tt", "gz", "u", "w", "e")]
+        stat = {n: tile(n, [P, G, H], F32) for n in ("sum_p", "sum_nxp", "zs", "rz", "nc_share", "gain")}
+
+        for g, h in tiles:
+            nc.scalar.activation(out=q[g, h][:], in_=banks[g][h][:], func=ACT.Sigmoid, scale=-1.0)
+        for t in tiles:
+            nc.scalar.activation(out=lnq[t][:], in_=q[t][:], func=ACT.Ln, bias=LN_FLOOR)
+        w2_b, w2_dst, w2_src = weight_views("w2_b", w2_raw)
+        nc.scalar.copy(out=w2_dst, in_=w2_src)
+
+        for g, h in tiles:
+            nc.vector.scalar_tensor_tensor(
+                out=nxp[g, h][:], in0=q[g, h][:], scalar=1.0, in1=banks[g][H + h][:],
+                op0=ALU.subtract, op1=ALU.mult, accum_out=stat["sum_nxp"][:, g, h : h + 1],
+            )
+
+        def softplus(g, h):
+            nc.vector.scalar_tensor_tensor(
+                out=p1[g, h][:], in0=lnq[g, h][:], scalar=-1.0, in1=banks[g][h][:],
+                op0=ALU.mult, op1=ALU.max, accum_out=stat["sum_p"][:, g, h : h + 1],
+            )
+
+        def denominators(g):
+            nc.vector.tensor_tensor(out=stat["zs"][:, g, :], in0=stat["sum_p"][:, g, :], in1=re_sb[:, g, :], op=ALU.add)
+
+        def inverses(g):
+            nc.vector.reciprocal(out=stat["rz"][:, g, :], in_=stat["zs"][:, g, :])
+
+        def row_factors(g):
+            nc.vector.tensor_tensor(out=stat["nc_share"][:, g, :], in0=stat["sum_nxp"][:, g, :], in1=stat["rz"][:, g, :], op=ALU.mult)
+            nc.vector.scalar_tensor_tensor(
+                out=stat["gain"][:, g, :], in0=stat["rz"][:, g, :], scalar=512.0, in1=og_sb[:, g, :], op0=ALU.mult, op1=ALU.mult
+            )
+
+        def centred(g, h):
+            nc.vector.scalar_tensor_tensor(
+                out=a1[g, h][:], in0=p1[g, h][:], scalar=stat["nc_share"][:, g, h : h + 1], in1=nxp[g, h][:],
+                op0=ALU.mult, op1=ALU.subtract,
+            )
+
+        softplus(0, 0)
+        softplus(0, 1)
+        softplus(1, 0)
+        denominators(0)
+        softplus(1, 1)
+        inverses(0)
+        denominators(1)
+        row_factors(0)
+        inverses(1)
+        centred(0, 0)
+        row_factors(1)
+        quantise(w2_mx, slice(0, M), w2_b)
+        centred(0, 1)
+        centred(1, 0)
+        centred(1, 1)
+
+        for t in tiles:
+            product(w2_mx, x_mx, H, [t])
+            product(w2_mx, dx_mx, 0, [t])
+
+        for g, h in tiles:
+            nc.scalar.activation(out=t2[g, h][:], in_=banks[g][H + h][:], func=ACT.Tanh)
+            nc.scalar.activation(out=tt[g, h][:], in_=t2[g, h][:], func=ACT.Square)
+
+        for g, h in tiles:
+            nc.vector.scalar_tensor_tensor(
+                out=gz[g, h][:], in0=p1[g, h][:], scalar=stat["gain"][:, g, h : h + 1], in1=banks[g][h][:],
+                op0=ALU.mult, op1=ALU.mult,
+            )
+
+        y = [tile("y%d" % g, [P, H, N], F32) for g in range(G)]
+        y_hbm = out_0.rearrange("(g q h) n -> g q h n", g=G, h=H)
+        words_hbm = out_1[0].rearrange("p n u -> p (n u)").bitcast(I32)
+        scales_hbm = out_2[0].bitcast(I32)
+
+        def terms(g):
+            for h in range(H):
+                nc.vector.scalar_tensor_tensor(
+                    out=u[g, h][:], in0=a1[g, h][:], scalar=stat["gain"][:, g, h : h + 1], in1=t2[g, h][:],
+                    op0=ALU.mult, op1=ALU.mult,
+                )
+            for h in range(H):
+                nc.vector.scalar_tensor_tensor(
+                    out=w[g, h][:], in0=tt[g, h][:], scalar=1.0, in1=gz[g, h][:], op0=ALU.subtract, op1=ALU.mult
+                )
+
+        def add_base(g):
+            for h in range(H):
+                nc.vector.tensor_tensor(out=e[g, h][:], in0=base_sb[:, g, h * N : (h + 1) * N], in1=w[g, h][:], op=ALU.subtract)
+
+        def result(g, cols):
+            for h in range(H):
+                nc.vector.tensor_tensor(out=y[g][:, h, cols], in0=e[g, h][:, cols], in1=u[g, h][:, cols], op=ALU.add)
+
+        pairs = {(g, a): tile("pairs%d%d" % (g, a), [P, HALF * H], BF16) for g in range(G) for a in range(2)}
+        moved = [tile("moved%d" % g, [P, 2, HALF], I32) for g in range(G)]
+        y_b = [tile("y_b%d" % g, [P, HALF * PACK], BF16) for g in range(G)]
+        y_mx = [mx_tiles("y%d" % g, HALF) for g in range(G)]
+
+        def round_pairs(copy, g, a):
+            copy(
+                out=pairs[g, a][:].rearrange("p (c i h) -> p c h i", i=4, h=H),
+                in_=y[g][:, :, halves[a]].rearrange("p h (c i) -> p c h i", i=4),
+            )
+
+        def move(queue, g, a):
+            queue.dma_start(out=moved[g][a * ROWS : (a + 1) * ROWS, :, :], in_=pairs[g, a][:].bitcast(I32))
+
+        def join_pairs(g):
+            nc.vector.tensor_copy(
+                out=y_b[g][:].bitcast(I32).rearrange("p (c i e) -> p c e i", i=4, e=2),
+                in_=moved[g][:].rearrange("p e (c i) -> p c e i", i=4),
+            )
+
+        def store_planes(g, queues):
+            codes, scales = y_mx[g]
+            for a in range(2):
+                queues[a].dma_start(
+                    out=words_hbm[g * ROWS : (g + 1) * ROWS, halves[a]],
+                    in_=codes[a * ROWS : (a + 1) * ROWS, :].bitcast(I32),
+                )
+            for a in range(2):
+                for b in range(2):
+                    first = a * ROWS + 32 * b
+                    row = 8 * g + 4 * b
+                    queues[b].dma_start(
+                        out=scales_hbm[row : row + 4, a * HALF // 4 : (a + 1) * HALF // 4],
+                        in_=scales[first : first + 4, :].bitcast(I32),
+                    )
+
+        terms(0)
+        add_base(0)
+        result(0, slice(0, N))
+        nc.sync.dma_start(out=y_hbm[0], in_=y[0][:])
+        for a in range(2):
+            round_pairs(nc.scalar.copy, 0, a)
+            move(nc.sync, 0, a)
+
+        terms(1)
+        add_base(1)
+        join_pairs(0)
+        result(1, halves[0])
+        quantise(y_mx[0], slice(0, HALF), y_b[0])
+        round_pairs(nc.scalar.copy, 1, 0)
+        move(nc.scalar, 1, 0)
+        nc.sync.dma_start(out=y_hbm[1][:, :, halves[0]], in_=y[1][:, :, halves[0]])
+        result(1, halves[1])
+        round_pairs(nc.vector.tensor_copy, 1, 1)
+        move(nc.sync, 1, 1)
+        nc.sync.dma_start(out=y_hbm[1][:, :, halves[1]], in_=y[1][:, :, halves[1]])
+        store_planes(0, [nc.scalar, nc.scalar])
+        join_pairs(1)
+        quantise(y_mx[1], slice(0, HALF), y_b[1])
+        store_planes(1, [nc.sync, nc.scalar])

@@ -47,8 +47,12 @@ def tile_rows_pl_tnrowshare_kernel(tc, x, w1, w2, re, dx, og, base, out_0, out_1
         nc.sync.dma_start(out=re_sb[:], in_=re.rearrange("g (q h) o -> q g (h o)", h=H))
         og_sb = tile("og_sb", [P, G, H], F32)
         nc.sync.dma_start(out=og_sb[:], in_=og.rearrange("g (q h) o -> q g (h o)", h=H))
-        base_sb = tile("base_sb", [P, G, H * N], F32)
-        nc.sync.dma_start(out=base_sb[:], in_=base.rearrange("g (q h) n -> q g (h n)", h=H))
+        halves = [slice(a * HALF, (a + 1) * HALF) for a in range(2)]
+        sides = [slice(a * ROWS, (a + 1) * ROWS) for a in range(2)]
+        base_sb = [tile("base%d" % g, [P, PACK, HALF], F32) for g in range(G)]
+        for g in range(G):
+            for a in range(2):
+                nc.sync.dma_start(out=base_sb[g][sides[a], :, :], in_=base[g].rearrange("(p t) n -> p t n", t=PACK)[:, :, halves[a]])
 
         def round_columns(name, raw, a):
             grouped = tile(name, [P, HALF * PACK], BF16)
@@ -72,8 +76,8 @@ def tile_rows_pl_tnrowshare_kernel(tc, x, w1, w2, re, dx, og, base, out_0, out_1
 
         banks = [[ps.tile([P, N], F32, name="bank%d%d" % (g, b), tag="bank%d%d" % (g, b)) for b in range(2 * H)] for g in range(G)]
 
-        def product(w_mx, x_mx, first_bank, which):
-            for g, h in which:
+        def product(w_mx, x_mx, first_bank):
+            for g, h in tiles:
                 rows = slice(g * ROWS, (g + 1) * ROWS)
                 cols = slice(h * P, (h + 1) * P)
                 nc.tensor.matmul_mx(
@@ -86,7 +90,6 @@ def tile_rows_pl_tnrowshare_kernel(tc, x, w1, w2, re, dx, og, base, out_0, out_1
                     stop=True,
                 )
 
-        halves = [slice(a * HALF, (a + 1) * HALF) for a in range(2)]
         x_mx, dx_mx = mx_tiles("x", N), mx_tiles("dx", N)
         w1_mx, w2_mx = mx_tiles("w1", M), mx_tiles("w2", M)
 
@@ -96,17 +99,17 @@ def tile_rows_pl_tnrowshare_kernel(tc, x, w1, w2, re, dx, og, base, out_0, out_1
         nc.vector.tensor_copy(out=w1_dst, in_=w1_src)
         quantise(x_mx, halves[1], x_b[1])
         quantise(w1_mx, slice(0, M), w1_b)
-        product(w1_mx, x_mx, 0, tiles)
+        product(w1_mx, x_mx, 0)
 
         dx_b = [round_columns("dx_b%d" % a, dx_raw, a) for a in range(2)]
         for a in range(2):
             quantise(dx_mx, halves[a], dx_b[a])
-        product(w1_mx, dx_mx, H, tiles)
+        product(w1_mx, dx_mx, H)
 
         def per_tile(name):
             return {t: tile("%s%d%d" % (name, t[0], t[1]), [P, N], F32) for t in tiles}
 
-        q, lnq, nxp, p1, a1, t2, tt, gz, u, w, e = [per_tile(n) for n in ("q", "lnq", "nxp", "p", "a", "t", "tt", "gz", "u", "w", "e")]
+        q, lnq, nxp, p1, a1, t2, tt, gz, u, w, v = [per_tile(n) for n in ("q", "lnq", "nxp", "p", "a", "t", "tt", "gz", "u", "w", "v")]
         stat = {n: tile(n, [P, G, H], F32) for n in ("sum_p", "sum_nxp", "zs", "rz", "nc_share", "gain")}
 
         for g, h in tiles:
@@ -162,13 +165,14 @@ def tile_rows_pl_tnrowshare_kernel(tc, x, w1, w2, re, dx, og, base, out_0, out_1
         centred(1, 0)
         centred(1, 1)
 
-        for t in tiles:
-            product(w2_mx, x_mx, H, [t])
-            product(w2_mx, dx_mx, 0, [t])
+        product(w2_mx, dx_mx, 0)
+        product(w2_mx, x_mx, H)
 
-        for g, h in tiles:
-            nc.scalar.activation(out=t2[g, h][:], in_=banks[g][H + h][:], func=ACT.Tanh)
-            nc.scalar.activation(out=tt[g, h][:], in_=t2[g, h][:], func=ACT.Square)
+        for g in range(G):
+            for h in range(H):
+                nc.scalar.activation(out=t2[g, h][:], in_=banks[g][H + h][:], func=ACT.Tanh)
+            for h in range(H):
+                nc.scalar.activation(out=tt[g, h][:], in_=t2[g, h][:], func=ACT.Square)
 
         for g, h in tiles:
             nc.vector.scalar_tensor_tensor(
@@ -176,10 +180,14 @@ def tile_rows_pl_tnrowshare_kernel(tc, x, w1, w2, re, dx, og, base, out_0, out_1
                 op0=ALU.mult, op1=ALU.mult,
             )
 
-        y = [tile("y%d" % g, [P, H, N], F32) for g in range(G)]
-        y_hbm = out_0.rearrange("(g q h) n -> g q h n", g=G, h=H)
+        moved = [tile("moved%d" % g, [P, PACK, HALF], F32) for g in range(G)]
+        y = [tile("y%d" % g, [P, PACK, HALF], F32) for g in range(G)]
+        y_b = [tile("y_b%d" % g, [P, HALF * PACK], BF16) for g in range(G)]
+        y_mx = [mx_tiles("y%d" % g, HALF) for g in range(G)]
+        y_hbm = out_0.rearrange("(g p t) n -> g p t n", g=G, t=PACK)
         words_hbm = out_1[0].rearrange("p n u -> p (n u)").bitcast(I32)
         scales_hbm = out_2[0].bitcast(I32)
+        queues = [nc.sync, nc.scalar]
 
         def terms(g):
             for h in range(H):
@@ -191,42 +199,31 @@ def tile_rows_pl_tnrowshare_kernel(tc, x, w1, w2, re, dx, og, base, out_0, out_1
                 nc.vector.scalar_tensor_tensor(
                     out=w[g, h][:], in0=tt[g, h][:], scalar=1.0, in1=gz[g, h][:], op0=ALU.subtract, op1=ALU.mult
                 )
-
-        def add_base(g):
             for h in range(H):
-                nc.vector.tensor_tensor(out=e[g, h][:], in0=base_sb[:, g, h * N : (h + 1) * N], in1=w[g, h][:], op=ALU.subtract)
+                nc.vector.tensor_tensor(out=v[g, h][:], in0=u[g, h][:], in1=w[g, h][:], op=ALU.subtract)
+                for a in range(2):
+                    nc.sync.dma_start(
+                        out=moved[g][sides[a], :, :].rearrange("p (e h) c -> p e h c", h=H)[:, :, h, :],
+                        in_=v[g, h][:, halves[a]],
+                    )
 
         def result(g, cols):
-            for h in range(H):
-                nc.vector.tensor_tensor(out=y[g][:, h, cols], in0=e[g, h][:, cols], in1=u[g, h][:, cols], op=ALU.add)
+            nc.vector.tensor_tensor(out=y[g][:, :, cols], in0=moved[g][:, :, cols], in1=base_sb[g][:, :, cols], op=ALU.add)
 
-        pairs = {(g, a): tile("pairs%d%d" % (g, a), [P, HALF * H], BF16) for g in range(G) for a in range(2)}
-        moved = [tile("moved%d" % g, [P, 2, HALF], I32) for g in range(G)]
-        y_b = [tile("y_b%d" % g, [P, HALF * PACK], BF16) for g in range(G)]
-        y_mx = [mx_tiles("y%d" % g, HALF) for g in range(G)]
+        def store_result(g):
+            for a in range(2):
+                queues[a].dma_start(out=y_hbm[g][:, :, halves[a]], in_=y[g][sides[a], :, :])
 
-        def round_pairs(copy, g, a):
+        def round_result(copy, g, cols):
             copy(
-                out=pairs[g, a][:].rearrange("p (c i h) -> p c h i", i=4, h=H),
-                in_=y[g][:, :, halves[a]].rearrange("p h (c i) -> p c h i", i=4),
+                out=y_b[g][:, cols.start * PACK : cols.stop * PACK].rearrange("p (c i t) -> p c t i", i=4, t=PACK),
+                in_=y[g][:, :, cols].rearrange("p t (c i) -> p c t i", i=4),
             )
 
-        def move(queue, g, a):
-            queue.dma_start(out=moved[g][a * ROWS : (a + 1) * ROWS, :, :], in_=pairs[g, a][:].bitcast(I32))
-
-        def join_pairs(g):
-            nc.vector.tensor_copy(
-                out=y_b[g][:].bitcast(I32).rearrange("p (c i e) -> p c e i", i=4, e=2),
-                in_=moved[g][:].rearrange("p e (c i) -> p c e i", i=4),
-            )
-
-        def store_planes(g, queues):
+        def store_planes(g):
             codes, scales = y_mx[g]
             for a in range(2):
-                queues[a].dma_start(
-                    out=words_hbm[g * ROWS : (g + 1) * ROWS, halves[a]],
-                    in_=codes[a * ROWS : (a + 1) * ROWS, :].bitcast(I32),
-                )
+                queues[a].dma_start(out=words_hbm[sides[g], halves[a]], in_=codes[sides[a], :].bitcast(I32))
             for a in range(2):
                 for b in range(2):
                     first = a * ROWS + 32 * b
@@ -236,27 +233,14 @@ def tile_rows_pl_tnrowshare_kernel(tc, x, w1, w2, re, dx, og, base, out_0, out_1
                         in_=scales[first : first + 4, :].bitcast(I32),
                     )
 
+        quarters = [slice(0, HALF // 2), slice(HALF // 2, HALF)]
         terms(0)
-        add_base(0)
-        result(0, slice(0, N))
-        nc.sync.dma_start(out=y_hbm[0], in_=y[0][:])
-        for a in range(2):
-            round_pairs(nc.scalar.copy, 0, a)
-            move(nc.sync, 0, a)
-
         terms(1)
-        add_base(1)
-        join_pairs(0)
-        result(1, halves[0])
-        quantise(y_mx[0], slice(0, HALF), y_b[0])
-        round_pairs(nc.scalar.copy, 1, 0)
-        move(nc.scalar, 1, 0)
-        nc.sync.dma_start(out=y_hbm[1][:, :, halves[0]], in_=y[1][:, :, halves[0]])
-        result(1, halves[1])
-        round_pairs(nc.vector.tensor_copy, 1, 1)
-        move(nc.sync, 1, 1)
-        nc.sync.dma_start(out=y_hbm[1][:, :, halves[1]], in_=y[1][:, :, halves[1]])
-        store_planes(0, [nc.scalar, nc.scalar])
-        join_pairs(1)
-        quantise(y_mx[1], slice(0, HALF), y_b[1])
-        store_planes(1, [nc.sync, nc.scalar])
+        for g in range(G):
+            result(g, quarters[0])
+            round_result(nc.scalar.copy, g, quarters[0])
+            result(g, quarters[1])
+            store_result(g)
+            round_result(nc.vector.tensor_copy, g, quarters[1])
+            quantise(y_mx[g], slice(0, HALF), y_b[g])
+            store_planes(g)

@@ -24,7 +24,7 @@ LN_FLOOR = 1e-12
 
 def tile_rows_pl_tnrowshare_kernel(tc, x, w1, w2, re, dx, og, base, out_0, out_1, out_2):
     nc = tc.nc
-    tiles = [(g, h) for g in range(G) for h in range(H)]
+    tiles = [(g, h) for h in range(H) for g in range(G)]
 
     with ExitStack() as ctx:
         sb = ctx.enter_context(tc.tile_pool(name="sb", bufs=1))
@@ -48,11 +48,9 @@ def tile_rows_pl_tnrowshare_kernel(tc, x, w1, w2, re, dx, og, base, out_0, out_1
         og_sb = tile("og_sb", [P, G, H], F32)
         nc.sync.dma_start(out=og_sb[:], in_=og.rearrange("g (q h) o -> q g (h o)", h=H))
         halves = [slice(a * HALF, (a + 1) * HALF) for a in range(2)]
-        sides = [slice(a * ROWS, (a + 1) * ROWS) for a in range(2)]
-        base_sb = [tile("base%d" % g, [P, PACK, HALF], F32) for g in range(G)]
-        for g in range(G):
-            for a in range(2):
-                nc.sync.dma_start(out=base_sb[g][sides[a], :, :], in_=base[g].rearrange("(p t) n -> p t n", t=PACK)[:, :, halves[a]])
+        base_sb = [tile("base%d" % a, [P, PACK, HALF], F32) for a in range(2)]
+        for a in range(2):
+            nc.sync.dma_start(out=base_sb[a][:], in_=base.rearrange("g (p t) n -> (g p) t n", t=PACK)[:, :, halves[a]])
 
         def round_columns(name, raw, a):
             grouped = tile(name, [P, HALF * PACK], BF16)
@@ -76,8 +74,8 @@ def tile_rows_pl_tnrowshare_kernel(tc, x, w1, w2, re, dx, og, base, out_0, out_1
 
         banks = [[ps.tile([P, N], F32, name="bank%d%d" % (g, b), tag="bank%d%d" % (g, b)) for b in range(2 * H)] for g in range(G)]
 
-        def product(w_mx, x_mx, first_bank):
-            for g, h in tiles:
+        def product(w_mx, x_mx, first_bank, which):
+            for g, h in which:
                 rows = slice(g * ROWS, (g + 1) * ROWS)
                 cols = slice(h * P, (h + 1) * P)
                 nc.tensor.matmul_mx(
@@ -99,148 +97,151 @@ def tile_rows_pl_tnrowshare_kernel(tc, x, w1, w2, re, dx, og, base, out_0, out_1
         nc.vector.tensor_copy(out=w1_dst, in_=w1_src)
         quantise(x_mx, halves[1], x_b[1])
         quantise(w1_mx, slice(0, M), w1_b)
-        product(w1_mx, x_mx, 0)
+        product(w1_mx, x_mx, 0, tiles)
 
         dx_b = [round_columns("dx_b%d" % a, dx_raw, a) for a in range(2)]
         for a in range(2):
             quantise(dx_mx, halves[a], dx_b[a])
-        product(w1_mx, dx_mx, H)
+        product(w1_mx, dx_mx, H, tiles)
+        w2_b, w2_dst, w2_src = weight_views("w2_b", w2_raw)
+        nc.vector.tensor_copy(out=w2_dst, in_=w2_src)
 
         def per_tile(name):
             return {t: tile("%s%d%d" % (name, t[0], t[1]), [P, N], F32) for t in tiles}
 
-        q, lnq, nxp, p1, a1, t2, tt, gz, u, w, v = [per_tile(n) for n in ("q", "lnq", "nxp", "p", "a", "t", "tt", "gz", "u", "w", "v")]
+        def per_pair(name):
+            return [tile("%s%d" % (name, h), [P, G, N], F32) for h in range(H)]
+
+        q, lnq, nxp, p1, a1, u, v = [per_tile(n) for n in ("q", "lnq", "nxp", "p", "a", "u", "v")]
+        t2, tt, gz, w = [per_pair(n) for n in ("t", "tt", "gz", "w")]
         stat = {n: tile(n, [P, G, H], F32) for n in ("sum_p", "sum_nxp", "zs", "rz", "nc_share", "gain")}
 
         for g, h in tiles:
             nc.scalar.activation(out=q[g, h][:], in_=banks[g][h][:], func=ACT.Sigmoid, scale=-1.0)
         for t in tiles:
             nc.scalar.activation(out=lnq[t][:], in_=q[t][:], func=ACT.Ln, bias=LN_FLOOR)
-        w2_b, w2_dst, w2_src = weight_views("w2_b", w2_raw)
-        nc.scalar.copy(out=w2_dst, in_=w2_src)
 
         for g, h in tiles:
             nc.vector.scalar_tensor_tensor(
                 out=nxp[g, h][:], in0=q[g, h][:], scalar=1.0, in1=banks[g][H + h][:],
                 op0=ALU.subtract, op1=ALU.mult, accum_out=stat["sum_nxp"][:, g, h : h + 1],
             )
-
-        def softplus(g, h):
+        quantise(w2_mx, slice(0, M), w2_b)
+        for g, h in tiles:
             nc.vector.scalar_tensor_tensor(
                 out=p1[g, h][:], in0=lnq[g, h][:], scalar=-1.0, in1=banks[g][h][:],
                 op0=ALU.mult, op1=ALU.max, accum_out=stat["sum_p"][:, g, h : h + 1],
             )
 
-        def denominators(g):
-            nc.vector.tensor_tensor(out=stat["zs"][:, g, :], in0=stat["sum_p"][:, g, :], in1=re_sb[:, g, :], op=ALU.add)
+        product(w2_mx, dx_mx, 0, tiles[:2])
+        product(w2_mx, x_mx, H, tiles[:1])
+        product(w2_mx, dx_mx, 0, tiles[2:])
+        product(w2_mx, x_mx, H, tiles[1:])
 
-        def inverses(g):
-            nc.vector.reciprocal(out=stat["rz"][:, g, :], in_=stat["zs"][:, g, :])
+        def scaled_direction(g, h):
+            nc.vector.tensor_tensor(out=gz[h][:, g, :], in0=p1[g, h][:], in1=banks[g][h][:], op=ALU.mult)
 
-        def row_factors(g):
-            nc.vector.tensor_tensor(out=stat["nc_share"][:, g, :], in0=stat["sum_nxp"][:, g, :], in1=stat["rz"][:, g, :], op=ALU.mult)
-            nc.vector.scalar_tensor_tensor(
-                out=stat["gain"][:, g, :], in0=stat["rz"][:, g, :], scalar=512.0, in1=og_sb[:, g, :], op0=ALU.mult, op1=ALU.mult
-            )
-
-        def centred(g, h):
+        scaled_direction(0, 0)
+        nc.vector.tensor_tensor(out=stat["zs"][:], in0=stat["sum_p"][:], in1=re_sb[:], op=ALU.add)
+        scaled_direction(1, 0)
+        nc.vector.reciprocal(out=stat["rz"][:], in_=stat["zs"][:])
+        scaled_direction(0, 1)
+        nc.vector.tensor_tensor(out=stat["nc_share"][:], in0=stat["sum_nxp"][:], in1=stat["rz"][:], op=ALU.mult)
+        nc.vector.scalar_tensor_tensor(
+            out=stat["gain"][:].rearrange("p g h -> p (g h)"), in0=stat["rz"][:].rearrange("p g h -> p (g h)"), scalar=512.0,
+            in1=og_sb[:].rearrange("p g h -> p (g h)"), op0=ALU.mult, op1=ALU.mult,
+        )
+        scaled_direction(1, 1)
+        for g, h in tiles:
             nc.vector.scalar_tensor_tensor(
                 out=a1[g, h][:], in0=p1[g, h][:], scalar=stat["nc_share"][:, g, h : h + 1], in1=nxp[g, h][:],
                 op0=ALU.mult, op1=ALU.subtract,
             )
 
-        softplus(0, 0)
-        softplus(0, 1)
-        softplus(1, 0)
-        denominators(0)
-        softplus(1, 1)
-        inverses(0)
-        denominators(1)
-        row_factors(0)
-        inverses(1)
-        centred(0, 0)
-        row_factors(1)
-        quantise(w2_mx, slice(0, M), w2_b)
-        centred(0, 1)
-        centred(1, 0)
-        centred(1, 1)
+        for h in range(H):
+            for g in range(G):
+                nc.scalar.activation(out=t2[h][:, g, :], in_=banks[g][H + h][:], func=ACT.Tanh)
+            nc.scalar.activation(out=tt[h][:], in_=t2[h][:], func=ACT.Square)
 
-        product(w2_mx, dx_mx, 0)
-        product(w2_mx, x_mx, H)
-
-        for g in range(G):
-            for h in range(H):
-                nc.scalar.activation(out=t2[g, h][:], in_=banks[g][H + h][:], func=ACT.Tanh)
-            for h in range(H):
-                nc.scalar.activation(out=tt[g, h][:], in_=t2[g, h][:], func=ACT.Square)
-
-        for g, h in tiles:
-            nc.vector.scalar_tensor_tensor(
-                out=gz[g, h][:], in0=p1[g, h][:], scalar=stat["gain"][:, g, h : h + 1], in1=banks[g][h][:],
-                op0=ALU.mult, op1=ALU.mult,
-            )
-
-        moved = [tile("moved%d" % g, [P, PACK, HALF], F32) for g in range(G)]
-        y = [tile("y%d" % g, [P, PACK, HALF], F32) for g in range(G)]
-        y_b = [tile("y_b%d" % g, [P, HALF * PACK], BF16) for g in range(G)]
-        y_mx = [mx_tiles("y%d" % g, HALF) for g in range(G)]
-        y_hbm = out_0.rearrange("(g p t) n -> g p t n", g=G, t=PACK)
+        moved = [tile("moved%d" % a, [P, PACK, HALF], F32) for a in range(2)]
+        y = [tile("y%d" % a, [P, PACK, HALF], F32) for a in range(2)]
+        y_b = [tile("y_b%d" % a, [P, HALF * PACK], BF16) for a in range(2)]
+        y_mx = mx_tiles("y", N)
+        y_hbm = out_0.rearrange("(p t) n -> p t n", t=PACK)
         words_hbm = out_1[0].rearrange("p n u -> p (n u)").bitcast(I32)
         scales_hbm = out_2[0].bitcast(I32)
-        queues = [nc.sync, nc.scalar]
 
-        def terms(g):
-            for h in range(H):
-                nc.vector.scalar_tensor_tensor(
-                    out=u[g, h][:], in0=a1[g, h][:], scalar=stat["gain"][:, g, h : h + 1], in1=t2[g, h][:],
-                    op0=ALU.mult, op1=ALU.mult,
-                )
-            for h in range(H):
-                nc.vector.scalar_tensor_tensor(
-                    out=w[g, h][:], in0=tt[g, h][:], scalar=1.0, in1=gz[g, h][:], op0=ALU.subtract, op1=ALU.mult
-                )
-            for h in range(H):
-                nc.vector.tensor_tensor(out=v[g, h][:], in0=u[g, h][:], in1=w[g, h][:], op=ALU.subtract)
-                for a in range(2):
-                    nc.sync.dma_start(
-                        out=moved[g][sides[a], :, :].rearrange("p (e h) c -> p e h c", h=H)[:, :, h, :],
-                        in_=v[g, h][:, halves[a]],
-                    )
+        def rows_of(ap, h):
+            return ap.rearrange("p (e h) c -> p e h c", h=H)[:, :, h, :]
 
-        def result(g, cols):
-            nc.vector.tensor_tensor(out=y[g][:, :, cols], in0=moved[g][:, :, cols], in1=base_sb[g][:, :, cols], op=ALU.add)
-
-        def store_result(g):
-            for a in range(2):
-                queues[a].dma_start(out=y_hbm[g][:, :, halves[a]], in_=y[g][sides[a], :, :])
-
-        def round_result(copy, g, cols):
-            copy(
-                out=y_b[g][:, cols.start * PACK : cols.stop * PACK].rearrange("p (c i t) -> p c t i", i=4, t=PACK),
-                in_=y[g][:, :, cols].rearrange("p t (c i) -> p c t i", i=4),
+        def share_term(g, h, a):
+            nc.vector.scalar_tensor_tensor(
+                out=u[g, h][:, halves[a]], in0=a1[g, h][:, halves[a]], scalar=stat["gain"][:, g, h : h + 1],
+                in1=t2[h][:, g, halves[a]], op0=ALU.mult, op1=ALU.mult,
             )
 
-        def store_planes(g):
-            codes, scales = y_mx[g]
-            for a in range(2):
-                queues[a].dma_start(out=words_hbm[sides[g], halves[a]], in_=codes[sides[a], :].bitcast(I32))
-            for a in range(2):
-                for b in range(2):
-                    first = a * ROWS + 32 * b
-                    row = 8 * g + 4 * b
-                    queues[b].dma_start(
-                        out=scales_hbm[row : row + 4, a * HALF // 4 : (a + 1) * HALF // 4],
-                        in_=scales[first : first + 4, :].bitcast(I32),
-                    )
+        def value_terms(h, a):
+            nc.vector.scalar_tensor_tensor(
+                out=w[h][:, :, halves[a]], in0=tt[h][:, :, halves[a]], scalar=1.0, in1=gz[h][:, :, halves[a]],
+                op0=ALU.subtract, op1=ALU.mult,
+            )
 
+        def change(g, h, a):
+            nc.vector.scalar_tensor_tensor(
+                out=v[g, h][:, halves[a]], in0=w[h][:, g, halves[a]], scalar=stat["gain"][:, g, h : h + 1],
+                in1=u[g, h][:, halves[a]], op0=ALU.mult, op1=ALU.subtract,
+            )
+            nc.sync.dma_start(out=rows_of(moved[a][g * ROWS : (g + 1) * ROWS, :, :], h), in_=v[g, h][:, halves[a]])
+
+        def result(a, h):
+            nc.vector.tensor_tensor(out=rows_of(y[a][:], h), in0=rows_of(base_sb[a][:], h), in1=rows_of(moved[a][:], h), op=ALU.subtract)
+            nc.sync.dma_start(out=rows_of(y_hbm[:, :, halves[a]], h), in_=rows_of(y[a][:], h))
+
+        def round_result(copy, a, cols):
+            copy(
+                out=y_b[a][:, cols.start * PACK : cols.stop * PACK].rearrange("p (c i t) -> p c t i", i=4, t=PACK),
+                in_=y[a][:, :, cols].rearrange("p t (c i) -> p c t i", i=4),
+            )
+
+        def quantise_result(a, cols):
+            first = a * HALF
+            nc.vector.quantize_mx(
+                out=y_mx[0][:, first + cols.start : first + cols.stop].bitcast(FP8X4),
+                scales=y_mx[1][:, first + cols.start : first + cols.stop],
+                in_=y_b[a][:, cols.start * PACK : cols.stop * PACK],
+            )
+
+        def store_words(a):
+            nc.sync.dma_start(out=words_hbm[:, halves[a]], in_=y_mx[0][:, halves[a]].bitcast(I32))
+
+        for a in range(2):
+            share_term(0, 0, a)
+            share_term(1, 0, a)
+            value_terms(0, a)
+            share_term(0, 1, a)
+            change(0, 0, a)
+            change(1, 0, a)
+            value_terms(1, a)
+            share_term(1, 1, a)
+            change(0, 1, a)
+            change(1, 1, a)
+
+        whole = slice(0, HALF)
         quarters = [slice(0, HALF // 2), slice(HALF // 2, HALF)]
-        terms(0)
-        terms(1)
-        for g in range(G):
-            result(g, quarters[0])
-            round_result(nc.scalar.copy, g, quarters[0])
-            result(g, quarters[1])
-            store_result(g)
-            round_result(nc.vector.tensor_copy, g, quarters[1])
-            quantise(y_mx[g], slice(0, HALF), y_b[g])
-            store_planes(g)
+        for a in range(2):
+            for h in range(H):
+                result(a, h)
+        round_result(nc.scalar.copy, 0, whole)
+        quantise_result(0, whole)
+        store_words(0)
+        round_result(nc.vector.tensor_copy, 1, quarters[0])
+        round_result(nc.scalar.copy, 1, quarters[1])
+        quantise_result(1, quarters[1])
+        quantise_result(1, quarters[0])
+        store_words(1)
+        for quadrant in range(4):
+            queue = nc.sync if quadrant == 3 else nc.scalar
+            queue.dma_start(
+                out=scales_hbm[4 * quadrant : 4 * quadrant + 4, :],
+                in_=y_mx[1][32 * quadrant : 32 * quadrant + 4, :].bitcast(I32),
+            )

from contextlib import ExitStack

import concourse.mybir as mybir

G, D, M, N = 2, 256, 256, 512
FLOPS = 4 * 2 * G * D * M * N

F32 = mybir.dt.float32
BF16 = mybir.dt.bfloat16
I32 = mybir.dt.int32
U32 = mybir.dt.uint32
U8 = mybir.dt.uint8
FP8X4 = mybir.dt.float8_e4m3fn_x4
ALU = mybir.AluOpType
ACT = mybir.ActivationFunctionType

P = 128
PACK = 4
ROWS = D // PACK
H = M // P
HALF = N // 2
LN_FLOOR = 1e-12


def tile_rows_pl_tnrowshare_kernel(tc, x, w1, w2, re, dx, og, base, out_0, out_1, out_2):
    nc = tc.nc
    tiles = [(g, h) for h in range(H) for g in range(G)]

    with ExitStack() as ctx:
        sb = ctx.enter_context(tc.tile_pool(name="sb", bufs=1))
        ps = ctx.enter_context(tc.psum_pool(name="ps", bufs=1))
        ctx.enter_context(tc.manual_schedule())

        def tile(name, shape, dtype):
            return sb.tile(shape, dtype, name=name, tag=name, align_bytes=64)

        def load_k_first(name, src, width):
            raw = tile(name, [P, PACK, width], F32)
            nc.sync.dma_start(out=raw[:], in_=src.rearrange("g (p j) w -> (g p) j w", j=PACK))
            return raw

        x_raw = load_k_first("x_raw", x, N)
        w1_raw = load_k_first("w1_raw", w1, M)
        dx_raw = load_k_first("dx_raw", dx, N)
        w2_raw = load_k_first("w2_raw", w2, M)
        re_sb = tile("re_sb", [P, G, H], F32)
        nc.sync.dma_start(out=re_sb[:], in_=re.rearrange("g (q h) o -> q g (h o)", h=H))
        og_sb = tile("og_sb", [P, G, H], F32)
        nc.sync.dma_start(out=og_sb[:], in_=og.rearrange("g (q h) o -> q g (h o)", h=H))
        halves = [slice(a * HALF, (a + 1) * HALF) for a in range(2)]
        base_sb = [tile("base%d" % a, [P, PACK, HALF], F32) for a in range(2)]
        for a in range(2):
            nc.sync.dma_start(out=base_sb[a][:], in_=base.rearrange("g (p t) n -> (g p) t n", t=PACK)[:, :, halves[a]])

        def round_columns(name, raw, a):
            grouped = tile(name, [P, HALF * PACK], BF16)
            nc.vector.tensor_copy(
                out=grouped[:].rearrange("p (c i j) -> p c j i", i=4, j=PACK),
                in_=raw[:, :, a * HALF : (a + 1) * HALF].rearrange("p j (c i) -> p c j i", i=4),
            )
            return grouped

        def weight_views(name, raw):
            grouped = tile(name, [P, M * PACK], BF16)
            dst = grouped[:].rearrange("p (h c i j) -> p c j i h", h=H, i=2, j=PACK)
            src = raw[:].rearrange("p j (c i h) -> p c j i h", i=2, h=H)
            return grouped, dst, src

        def mx_tiles(name, width):
            return tile(name + "_codes", [P, width], U32), tile(name + "_scales", [P, width], U8)

        def quantise(mx, cols, grouped):
            nc.vector.quantize_mx(out=mx[0][:, cols].bitcast(FP8X4), scales=mx[1][:, cols], in_=grouped[:])

        banks = [[ps.tile([P, N], F32, name="bank%d%d" % (g, b), tag="bank%d%d" % (g, b)) for b in range(2 * H)] for g in range(G)]

        def product(w_mx, x_mx, first_bank, which):
            for g, h in which:
                rows = slice(g * ROWS, (g + 1) * ROWS)
                cols = slice(h * P, (h + 1) * P)
                nc.tensor.matmul_mx(
                    out=banks[g][first_bank + h][:],
                    lhsT=w_mx[0][rows, cols].bitcast(FP8X4),
                    lhsT_scale=w_mx[1][rows, cols],
                    rhs=x_mx[0][rows, :].bitcast(FP8X4),
                    rhs_scale=x_mx[1][rows, :],
                    start=True,
                    stop=True,
                )

        x_mx, dx_mx = mx_tiles("x", N), mx_tiles("dx", N)
        w1_mx, w2_mx = mx_tiles("w1", M), mx_tiles("w2", M)

        x_b = [round_columns("x_b%d" % a, x_raw, a) for a in range(2)]
        quantise(x_mx, halves[0], x_b[0])
        w1_b, w1_dst, w1_src = weight_views("w1_b", w1_raw)
        nc.vector.tensor_copy(out=w1_dst, in_=w1_src)
        quantise(x_mx, halves[1], x_b[1])
        quantise(w1_mx, slice(0, M), w1_b)
        product(w1_mx, x_mx, 0, tiles)

        dx_b = [round_columns("dx_b%d" % a, dx_raw, a) for a in range(2)]
        for a in range(2):
            quantise(dx_mx, halves[a], dx_b[a])
        product(w1_mx, dx_mx, H, tiles)
        w2_b, w2_dst, w2_src = weight_views("w2_b", w2_raw)
        nc.vector.tensor_copy(out=w2_dst, in_=w2_src)

        def per_tile(name):
            return {t: tile("%s%d%d" % (name, t[0], t[1]), [P, N], F32) for t in tiles}

        def per_pair(name):
            return [tile("%s%d" % (name, h), [P, G, N], F32) for h in range(H)]

        q, lnq, nxp, p1, a1, u, v = [per_tile(n) for n in ("q", "lnq", "nxp", "p", "a", "u", "v")]
        t2, tt, gz, w = [per_pair(n) for n in ("t", "tt", "gz", "w")]
        stat = {n: tile(n, [P, G, H], F32) for n in ("sum_p", "sum_nxp", "zs", "rz", "nc_share", "gain")}

        for g, h in tiles:
            nc.scalar.activation(out=q[g, h][:], in_=banks[g][h][:], func=ACT.Sigmoid, scale=-1.0)
        for t in tiles:
            nc.scalar.activation(out=lnq[t][:], in_=q[t][:], func=ACT.Ln, bias=LN_FLOOR)

        for g, h in tiles:
            nc.vector.scalar_tensor_tensor(
                out=nxp[g, h][:], in0=q[g, h][:], scalar=1.0, in1=banks[g][H + h][:],
                op0=ALU.subtract, op1=ALU.mult, accum_out=stat["sum_nxp"][:, g, h : h + 1],
            )
        quantise(w2_mx, slice(0, M), w2_b)
        for g, h in tiles:
            nc.vector.scalar_tensor_tensor(
                out=p1[g, h][:], in0=lnq[g, h][:], scalar=-1.0, in1=banks[g][h][:],
                op0=ALU.mult, op1=ALU.max, accum_out=stat["sum_p"][:, g, h : h + 1],
            )

        product(w2_mx, dx_mx, 0, tiles[:2])
        product(w2_mx, x_mx, H, tiles[:1])
        product(w2_mx, dx_mx, 0, tiles[2:])
        product(w2_mx, x_mx, H, tiles[1:])

        def scaled_direction(g, h):
            nc.vector.tensor_tensor(out=gz[h][:, g, :], in0=p1[g, h][:], in1=banks[g][h][:], op=ALU.mult)

        scaled_direction(0, 0)
        nc.vector.tensor_tensor(out=stat["zs"][:], in0=stat["sum_p"][:], in1=re_sb[:], op=ALU.add)
        scaled_direction(1, 0)
        nc.vector.reciprocal(out=stat["rz"][:], in_=stat["zs"][:])
        scaled_direction(0, 1)
        nc.vector.tensor_tensor(out=stat["nc_share"][:], in0=stat["sum_nxp"][:], in1=stat["rz"][:], op=ALU.mult)
        nc.vector.scalar_tensor_tensor(
            out=stat["gain"][:].rearrange("p g h -> p (g h)"), in0=stat["rz"][:].rearrange("p g h -> p (g h)"), scalar=512.0,
            in1=og_sb[:].rearrange("p g h -> p (g h)"), op0=ALU.mult, op1=ALU.mult,
        )
        scaled_direction(1, 1)
        for g, h in tiles:
            nc.vector.scalar_tensor_tensor(
                out=a1[g, h][:], in0=p1[g, h][:], scalar=stat["nc_share"][:, g, h : h + 1], in1=nxp[g, h][:],
                op0=ALU.mult, op1=ALU.subtract,
            )

        for h in range(H):
            for g in range(G):
                nc.scalar.activation(out=t2[h][:, g, :], in_=banks[g][H + h][:], func=ACT.Tanh)
            nc.scalar.activation(out=tt[h][:], in_=t2[h][:], func=ACT.Square)

        moved = [tile("moved%d" % a, [P, PACK, HALF], F32) for a in range(2)]
        y = [tile("y%d" % a, [P, PACK, HALF], F32) for a in range(2)]
        y_b = [tile("y_b%d" % a, [P, HALF * PACK], BF16) for a in range(2)]
        y_mx = mx_tiles("y", N)
        y_hbm = out_0.rearrange("(p t) n -> p t n", t=PACK)
        words_hbm = out_1[0].rearrange("p n u -> p (n u)").bitcast(I32)
        scales_hbm = out_2[0].bitcast(I32)

        def rows_of(ap, h):
            return ap.rearrange("p (e h) c -> p e h c", h=H)[:, :, h, :]

        def share_term(g, h, a):
            nc.vector.scalar_tensor_tensor(
                out=u[g, h][:, halves[a]], in0=a1[g, h][:, halves[a]], scalar=stat["gain"][:, g, h : h + 1],
                in1=t2[h][:, g, halves[a]], op0=ALU.mult, op1=ALU.mult,
            )

        def value_terms(h, a):
            nc.vector.scalar_tensor_tensor(
                out=w[h][:, :, halves[a]], in0=tt[h][:, :, halves[a]], scalar=1.0, in1=gz[h][:, :, halves[a]],
                op0=ALU.subtract, op1=ALU.mult,
            )

        def change(g, h, a):
            nc.vector.scalar_tensor_tensor(
                out=v[g, h][:, halves[a]], in0=w[h][:, g, halves[a]], scalar=stat["gain"][:, g, h : h + 1],
                in1=u[g, h][:, halves[a]], op0=ALU.mult, op1=ALU.subtract,
            )
            nc.sync.dma_start(out=rows_of(moved[a][g * ROWS : (g + 1) * ROWS, :, :], h), in_=v[g, h][:, halves[a]])

        def result(a, h):
            nc.vector.tensor_tensor(out=rows_of(y[a][:], h), in0=rows_of(base_sb[a][:], h), in1=rows_of(moved[a][:], h), op=ALU.subtract)
            nc.sync.dma_start(out=rows_of(y_hbm[:, :, halves[a]], h), in_=rows_of(y[a][:], h))

        def round_result(copy, a, cols):
            copy(
                out=y_b[a][:, cols.start * PACK : cols.stop * PACK].rearrange("p (c i t) -> p c t i", i=4, t=PACK),
                in_=y[a][:, :, cols].rearrange("p t (c i) -> p c t i", i=4),
            )

        def quantise_result(a, cols):
            first = a * HALF
            nc.vector.quantize_mx(
                out=y_mx[0][:, first + cols.start : first + cols.stop].bitcast(FP8X4),
                scales=y_mx[1][:, first + cols.start : first + cols.stop],
                in_=y_b[a][:, cols.start * PACK : cols.stop * PACK],
            )

        def store_words(a):
            nc.sync.dma_start(out=words_hbm[:, halves[a]], in_=y_mx[0][:, halves[a]].bitcast(I32))

        for a in range(2):
            share_term(0, 0, a)
            share_term(1, 0, a)
            value_terms(0, a)
            share_term(0, 1, a)
            change(0, 0, a)
            change(1, 0, a)
            value_terms(1, a)
            share_term(1, 1, a)
            change(0, 1, a)
            change(1, 1, a)

        whole = slice(0, HALF)
        quarters = [slice(0, HALF // 2), slice(HALF // 2, HALF)]
        for a in range(2):
            for h in range(H):
                result(a, h)
        round_result(nc.scalar.copy, 0, whole)
        quantise_result(0, whole)
        store_words(0)
        round_result(nc.vector.tensor_copy, 1, quarters[0])
        round_result(nc.scalar.copy, 1, quarters[1])
        quantise_result(1, quarters[1])
        quantise_result(1, quarters[0])
        store_words(1)
        for quadrant in range(4):
            queue = nc.sync if quadrant == 3 else nc.scalar
            queue.dma_start(
                out=scales_hbm[4 * quadrant : 4 * quadrant + 4, :],
                in_=y_mx[1][32 * quadrant : 32 * quadrant + 4, :].bitcast(I32),
            )
